import numpy as np
import ml_dtypes


def mxq(x, axis, fmt="e4m3"):
    dtype, down = {"e4m3": (ml_dtypes.float8_e4m3fn, 7), "e5m2": (ml_dtypes.float8_e5m2, 14)}[fmt]
    v = np.moveaxis(np.asarray(x, np.float32).astype(ml_dtypes.bfloat16).astype(np.float64), axis, -1)
    blocks = v.reshape(v.shape[:-1] + (-1, 32))
    amax = np.abs(blocks).max(-1, keepdims=True)
    byte = np.maximum(np.where(amax > 0, np.frexp(amax)[1] - 1 + 127, 0) - down, 1)
    scale = np.exp2(byte - 127.0)
    codes = (blocks / scale).astype(np.float32).astype(dtype).astype(np.float64)
    return np.moveaxis((codes * scale).reshape(v.shape), -1, axis)


WIDE = False


def mx_kscale(k):
    if not WIDE:
        return np.ones(k)
    levels = np.array([10, -10, 5, -5, 0])
    if k % 512:
        return np.exp2(np.random.permutation(np.resize(levels, k // 32))).repeat(32)
    a = np.empty((k // 512, 16))
    for p in range(k // 512):
        a[p, :8] = np.random.permutation(np.resize(levels, 8))
        for g in range(8):
            far = levels[np.abs(levels - a[p, g]) >= 10]
            a[p, g + 8] = far[np.random.randint(len(far))]
    return np.exp2(a.ravel()).repeat(32)


def f64(x):
    return np.asarray(x).astype(np.float64)


def striped(idx):
    return np.tile(idx.reshape(-1, 16).T, (8, 1)).astype(np.uint16)


def unstriped(offs):
    return offs[:16].T.reshape(-1).astype(np.int64)


E2M1 = np.array([0.0, 0.5, 1.0, 1.5, 2.0, 3.0, 4.0, 6.0, -0.0, -0.5, -1.0, -1.5, -2.0, -3.0, -4.0, -6.0])


def pack_weight(w, fmt):
    k, n = w.shape
    w = f64(np.asarray(w, np.float32).astype(ml_dtypes.bfloat16)).reshape(k // 32, 32, n)
    amax = np.abs(w).max(1)
    if fmt == "e4m3":
        byte = np.frexp(amax)[1] - 1 + 127 - 7
    else:
        mant, ex = np.frexp(amax / 6.0)
        byte = np.where(mant > 0.5, ex, ex - 1) + 127
    byte = np.clip(np.where(amax > 0, byte, 1), 1, 254)
    scaled = (w * np.exp2(127.0 - byte)[:, None, :]).reshape(k, n).astype(np.float32)
    by_word = np.ascontiguousarray(scaled.reshape(k // 512, 128, 4, n).transpose(0, 1, 3, 2))
    if fmt == "e4m3":
        words = by_word.astype(ml_dtypes.float8_e4m3fn).view(np.uint8)
    else:
        c = by_word.astype(ml_dtypes.float4_e2m1fn).view(np.uint8) & 0xF
        words = (c[..., 0::2] | (c[..., 1::2] << 4)).reshape(k // 512, 128, 2 * n)
    return np.ascontiguousarray(words), np.ascontiguousarray(byte.astype(np.uint8).reshape(k // 512, 16, n))


def unpack_weight(words, scales, fmt):
    g, _, n = scales.shape
    words = np.ascontiguousarray(words).reshape(g, 128, n, -1)
    if fmt == "e4m3":
        vals = words.view(ml_dtypes.float8_e4m3fn).astype(np.float64)
    else:
        nib = np.empty((g, 128, n, 4), np.uint8)
        nib[..., 0::2] = words & 0xF
        nib[..., 1::2] = words >> 4
        vals = E2M1[nib]
    vals = vals * np.repeat(np.exp2(scales.astype(np.float64) - 127.0), 8, axis=1)[..., None]
    return vals.transpose(0, 1, 3, 2).reshape(g * 512, n)


def gelu(v):
    return 0.5 * v * (1.0 + np.tanh(np.sqrt(2.0 / np.pi) * (v + 0.044715 * v**3)))


K, T, S, H, P = 1024, 4096, 1024, 1024, 512


def setup_inputs():
    n = np.random.standard_normal
    s = mx_kscale(K)[:, None]
    u = mx_kscale(H)[:, None]
    tab_words, tab_scales = pack_weight(n((K, T)) * s, "e4m3")
    w1 = (0.52 * n((K, H)) / np.sqrt(K) / s).astype(np.float32)
    w4_words, w4_scales = pack_weight(1.3 * n((K, H)) / np.sqrt(K) / s, "e2m1")
    gain = (np.exp(0.3 * n(H)) * u[:, 0]).astype(np.float32)
    worth = (2.0 * np.exp(0.3 * n(H)) / np.sqrt(H) / u[:, 0] ** 2).astype(np.float32)
    shared = np.exp(0.4 * n((P, P))).astype(np.float32)
    offs = striped(np.random.permutation(T)[:S])
    pos1 = striped(np.random.permutation(S)[:P])
    pos2 = striped(np.random.permutation(S)[:P])
    return {"tab_words": tab_words, "tab_scales": tab_scales, "w1": w1,
            "w4_words": w4_words, "w4_scales": w4_scales, "gain": gain,
            "worth": worth, "shared": shared,
            "offs": offs, "pos1": pos1, "pos2": pos2}


def reference(tab_words, tab_scales, w1, w4_words, w4_scales, gain, worth, shared, offs, pos1, pos2):
    v = unpack_weight(tab_words, tab_scales, "e4m3")[:, unstriped(offs)]
    w4 = unpack_weight(w4_words, w4_scales, "e2m1")
    a = mxq(f64(w1), 0, "e4m3").T @ v
    b = w4.T @ v
    h = np.cos(a) * np.tanh(b) * f64(gain)[:, None]
    x1 = h[:, unstriped(pos1)]
    x2 = np.abs(h[:, unstriped(pos2)]) * f64(worth)[:, None]
    e = mxq(x1, 0, "e4m3").T @ mxq(x2, 0, "e4m3")
    return e * f64(shared)

@@ -1,0 +1,304 @@
+import math
+from contextlib import ExitStack
+
+import concourse.mybir as mybir
+from concourse.masks import make_identity
+
+K, T, S, H, PAIRS = 1024, 4096, 1024, 1024, 512
+FLOPS = 2 * (2 * K * H * S + H * PAIRS * PAIRS)
+
+F32 = mybir.dt.float32
+BF16 = mybir.dt.bfloat16
+I32 = mybir.dt.int32
+U32 = mybir.dt.uint32
+U16 = mybir.dt.uint16
+U8 = mybir.dt.uint8
+FP8X4 = mybir.dt.float8_e4m3fn_x4
+FP4X4 = mybir.dt.float4_e2m1fn_x4
+ALU = mybir.AluOpType
+ACT = mybir.ActivationFunctionType
+
+P = 128
+PACK = 4
+PASS = P * PACK
+K_PASSES = K // PASS
+H_PASSES = H // PASS
+ROW_TILES = H // P
+BANK = 512
+HALVES = S // BANK
+RUN = 8
+GROUPS = P // RUN
+ALIGN = 64
+TURN = 1.0 / (2.0 * math.pi)
+VECTOR_REDUCED = 3
+
+
+def tile_list_softplay_pair_grid_kernel(
+    tc, tab_words, tab_scales, w1, w4_words, w4_scales, gain, worth, shared, offs, pos1, pos2, out
+):
+    nc = tc.nc
+    with ExitStack() as ctx:
+        lists = ctx.enter_context(tc.tile_pool(name="lists", bufs=1))
+        keep = ctx.enter_context(tc.tile_pool(name="keep", bufs=1))
+        ring = ctx.enter_context(tc.tile_pool(name="ring", bufs=2))
+        psum = ctx.enter_context(tc.psum_pool(name="psum", bufs=4))
+
+        offs_sb = lists.tile([P, S // 16], U16, name="offs_sb")
+        pos1_sb = lists.tile([P, PAIRS // 16], U16, name="pos1_sb")
+        pos2_sb = lists.tile([P, PAIRS // 16], U16, name="pos2_sb")
+        nc.sync.dma_start(offs_sb[:], offs)
+        nc.sync.dma_start(pos1_sb[:], pos1)
+        nc.sync.dma_start(pos2_sb[:], pos2)
+
+        def staging(slot, shape, dtype, name):
+            return keep.tile(shape, dtype, name=name, tag="staging%d" % slot, align_bytes=ALIGN)
+
+        tab_sc = staging(1, [P, K_PASSES, T], U8, "tab_sc")
+        nc.vector.memset(tab_sc[:].rearrange("p a t -> p (a t)").bitcast(I32), 0)
+        w4_sc_raw = keep.tile([P, K_PASSES, H], U8, name="w4_sc_raw", align_bytes=ALIGN)
+        nc.vector.memset(w4_sc_raw[:].rearrange("p a c -> p (a c)").bitcast(I32), 0)
+        vec_rows = keep.tile([P, H_PASSES * P], F32, name="vec_rows")
+        nc.vector.memset(vec_rows[:], 0.0)
+
+        w4_raw = staging(0, [P, K_PASSES, H // 2], I32, "w4_raw")
+        nc.sync.dma_start(w4_raw[:], w4_words.rearrange("a p n -> p a n").bitcast(I32))
+        tab = {}
+
+        def load_table(a, slot):
+            tab[a] = staging(slot, [P, T], I32, "tab%d" % a)
+            nc.sync.dma_start(tab[a][:], tab_words[a].rearrange("p t i -> p (t i)").bitcast(I32))
+
+        load_table(0, 2)
+        for q in range(4):
+            nc.scalar.dma_start(
+                tab_sc[32 * q : 32 * q + 4, :, :].bitcast(I32),
+                tab_scales[:, 4 * q : 4 * q + 4, :].rearrange("a r t -> r a t").bitcast(I32),
+            )
+        for q in range(4):
+            (nc.gpsimd if q < 2 else nc.scalar).dma_start(
+                w4_sc_raw[32 * q : 32 * q + 4, :, :].bitcast(I32),
+                w4_scales[:, 4 * q : 4 * q + 4, :].rearrange("a r c -> r a c").bitcast(I32),
+            )
+        for v, vec in enumerate((gain, worth)):
+            nc.gpsimd.dma_start(
+                vec_rows[PACK * v : PACK * (v + 1), :].rearrange("t (g e) -> t g e", e=RUN),
+                vec.rearrange("(g t e) -> t g e", t=PACK, e=RUN),
+            )
+        ident = keep.tile([P, P], F32, name="ident")
+        make_identity(nc, ident[:])
+
+        w4_codes = keep.tile([P, K_PASSES, H // 2], I32, name="w4_codes", align_bytes=ALIGN)
+        nc.vector.tensor_copy(
+            w4_codes[:].rearrange("p a (b t g w) -> p (a b) t g w", b=H_PASSES, t=PACK, g=GROUPS),
+            w4_raw[:].rearrange("p a (b g t w) -> p (a b) t g w", b=H_PASSES, t=PACK, g=GROUPS),
+        )
+
+        load_table(1, 0)
+
+        v_sc = [keep.tile([P, S], U8, name="v_sc%d" % a, align_bytes=ALIGN) for a in range(K_PASSES)]
+        for a in range(K_PASSES):
+            nc.vector.tensor_copy(v_sc[a][:], tab_sc[:, a, :].indirect(offs_sb[:]))
+
+        w4_sc = keep.tile([P, K_PASSES, H], U8, name="w4_sc", align_bytes=ALIGN)
+        nc.vector.tensor_copy(
+            w4_sc[:].bitcast(I32).rearrange("p a (b t g w) -> p (a b) t g w", b=H_PASSES, t=PACK, g=GROUPS),
+            w4_sc_raw[:].bitcast(I32).rearrange("p a (b g t w) -> p (a b) t g w", b=H_PASSES, t=PACK, g=GROUPS),
+        )
+
+        v_codes = {}
+        for a in range(K_PASSES):
+            for hf in range(HALVES):
+                v_codes[a, hf] = keep.tile([P, BANK], U32, name="v_codes%d%d" % (a, hf), align_bytes=ALIGN)
+                cols = slice(hf * BANK // 16, (hf + 1) * BANK // 16)
+                nc.vector.tensor_copy(v_codes[a, hf][:], tab[a][:].bitcast(U32).indirect(offs_sb[:, cols]))
+
+        w1_raw = {}
+
+        def load_w1(a, b, slot):
+            w1_raw[a, b] = staging(slot, [P, PACK, PASS], F32, "w1_raw%d%d" % (a, b))
+            nc.sync.dma_start(
+                w1_raw[a, b][:],
+                w1[a * PASS : (a + 1) * PASS, b * PASS : (b + 1) * PASS].rearrange("(p j) c -> p j c", j=PACK),
+            )
+
+        load_w1(0, 0, 1)
+        load_w1(1, 0, 2)
+        load_w1(1, 1, 0)
+        w1_codes = {}
+        w1_sc = {}
+
+        def round_w1(a, b, copy):
+            grouped = ring.tile([P, PASS * PACK], BF16, name="w1_grouped", align_bytes=ALIGN)
+            copy(
+                grouped[:].rearrange("p (t g e j) -> p t g e j", t=PACK, g=GROUPS, e=RUN),
+                w1_raw[a, b][:].rearrange("p j (g t e) -> p t g e j", t=PACK, e=RUN),
+            )
+            return grouped
+
+        def quantise_w1(a, b, grouped):
+            w1_codes[a, b] = keep.tile([P, PASS], U32, name="w1_codes%d%d" % (a, b), align_bytes=ALIGN)
+            w1_sc[a, b] = keep.tile([P, PASS], U8, name="w1_sc%d%d" % (a, b), align_bytes=ALIGN)
+            nc.vector.quantize_mx(out=w1_codes[a, b][:].bitcast(FP8X4), scales=w1_sc[a, b][:], in_=grouped[:])
+
+        tanh_b = []
+        for i in range(ROW_TILES):
+            th = keep.tile([P, S], F32, name="tanh_b%d" % i)
+            tanh_b.append(th)
+            for hf in range(HALVES):
+                acc = psum.tile([P, BANK], F32, name="b_ps", tag="shared_bank")
+                for a in range(K_PASSES):
+                    nc.tensor.matmul_mx(
+                        out=acc[:],
+                        lhsT=w4_codes[:, a, i * P // 2 : (i + 1) * P // 2].bitcast(U8).bitcast(FP4X4),
+                        lhsT_scale=w4_sc[:, a, i * P : (i + 1) * P],
+                        rhs=v_codes[a, hf][:].bitcast(FP8X4),
+                        rhs_scale=v_sc[a][:, hf * BANK : (hf + 1) * BANK],
+                        start=(a == 0),
+                        stop=(a == K_PASSES - 1),
+                    )
+                nc.scalar.activation(th[:, hf * BANK : (hf + 1) * BANK], acc[:], ACT.Tanh)
+
+        vec_ps = psum.tile([P, H_PASSES, P], F32, name="vec_ps", tag="shared_bank")
+        for b in range(H_PASSES):
+            nc.tensor.transpose(vec_ps[:, b, :], vec_rows[:, b * P : (b + 1) * P], ident[:])
+        vecs = keep.tile([P, H_PASSES, 2 * PACK], F32, name="vecs")
+        nc.vector.tensor_copy(vecs[:], vec_ps[:, :, 0 : 2 * PACK])
+
+        for a in range(K_PASSES):
+            quantise_w1(a, 0, round_w1(a, 0, nc.vector.tensor_copy))
+
+        load_w1(0, 1, 1)
+        shared_sb = staging(2, [P, PAIRS // P, PAIRS], F32, "shared_sb")
+        nc.sync.dma_start(shared_sb[:], shared.rearrange("(mt p) j -> p mt j", p=P))
+
+        cos_a = {}
+
+        def cosine(i):
+            b, t = divmod(i, PACK)
+            turns = ring.tile([P, S], F32, name="turns", bufs=4)
+            whole = ring.tile([P, S], I32, name="whole")
+            accs = []
+            for hf in range(HALVES):
+                acc = psum.tile([P, BANK], F32, name="a_ps")
+                accs.append(acc)
+                for a in range(K_PASSES):
+                    nc.tensor.matmul_mx(
+                        out=acc[:],
+                        lhsT=w1_codes[a, b][:, t * P : (t + 1) * P].bitcast(FP8X4),
+                        lhsT_scale=w1_sc[a, b][:, t * P : (t + 1) * P],
+                        rhs=v_codes[a, hf][:].bitcast(FP8X4),
+                        rhs_scale=v_sc[a][:, hf * BANK : (hf + 1) * BANK],
+                        start=(a == 0),
+                        stop=(a == K_PASSES - 1),
+                    )
+            if i < VECTOR_REDUCED:
+                for hf in range(HALVES):
+                    cols = slice(hf * BANK, (hf + 1) * BANK)
+                    nc.vector.tensor_scalar(whole[:, cols], accs[hf][:], TURN, 0.25, ALU.mult, ALU.add)
+                for hf in range(HALVES):
+                    cols = slice(hf * BANK, (hf + 1) * BANK)
+                    nc.vector.scalar_tensor_tensor(
+                        turns[:, cols], accs[hf][:], TURN, whole[:, cols], ALU.mult, ALU.subtract
+                    )
+                nc.scalar.activation(turns[:], turns[:], ACT.Sin, bias=math.pi / 2.0, scale=2.0 * math.pi)
+            else:
+                for hf in range(HALVES):
+                    cols = slice(hf * BANK, (hf + 1) * BANK)
+                    nc.scalar.activation(turns[:, cols], accs[hf][:], ACT.Copy, bias=0.25, scale=TURN)
+                nc.vector.tensor_copy(whole[:], turns[:])
+                nc.vector.tensor_tensor(turns[:], turns[:], whole[:], ALU.subtract)
+                nc.scalar.activation(turns[:], turns[:], ACT.Sin, scale=2.0 * math.pi)
+            cos_a[i] = turns
+
+        h = {}
+
+        def combine(i):
+            b, t = divmod(i, PACK)
+            h[i] = ring.tile([P, S], F32, name="h")
+            nc.vector.scalar_tensor_tensor(
+                h[i][:], cos_a[i][:], vecs[:, b, t : t + 1], tanh_b[i][:], ALU.mult, ALU.mult
+            )
+
+        x1_planes = {}
+        x2_planes = {}
+        x1_grouped = {}
+        x2_grouped = {}
+
+        def interleave(grouped, planes, first, end, copy):
+            copy(
+                grouped[:].rearrange("p (c i t) -> p c t i", i=4, t=PACK)[:, :, first:end, :],
+                planes[:, first:end, :].rearrange("p t (c i) -> p c t i", i=4),
+            )
+
+        def pick(i):
+            b, t = divmod(i, PACK)
+            last = b == H_PASSES - 1
+            if t == 0:
+                x1_planes[b] = ring.tile([P, PACK, PAIRS], BF16, name="x1_planes")
+                x2_planes[b] = ring.tile([P, PACK, PAIRS], BF16, name="x2_planes")
+                x1_grouped[b] = ring.tile([P, PAIRS * PACK], BF16, name="x1_grouped", align_bytes=ALIGN, bufs=1)
+                x2_grouped[b] = ring.tile([P, PAIRS * PACK], BF16, name="x2_grouped", align_bytes=ALIGN, bufs=1)
+            picked = ring.tile([P, PAIRS], F32, name="picked")
+            nc.vector.tensor_copy(picked[:], h[i][:].indirect(pos2_sb[:]))
+            nc.vector.tensor_copy(x1_planes[b][:, t, :], h[i][:].indirect(pos1_sb[:]))
+            nc.scalar.activation(picked[:], picked[:], ACT.Abs)
+            if last and t == PACK - 1:
+                x2_out = x2_grouped[b][:].rearrange("p (c t) -> p t c", t=PACK)[:, t, :]
+            else:
+                x2_out = x2_planes[b][:, t, :]
+            nc.scalar.activation(x2_out, picked[:], ACT.Copy, scale=vecs[:, b, PACK + t : PACK + t + 1])
+            if not last and t == PACK - 1:
+                interleave(x2_grouped[b], x2_planes[b], 0, PACK, nc.scalar.copy)
+                interleave(x1_grouped[b], x1_planes[b], 0, PACK, nc.scalar.copy)
+            if last and t == 1:
+                interleave(x1_grouped[b], x1_planes[b], 0, 2, nc.scalar.copy)
+            if last and t == 2:
+                interleave(x2_grouped[b], x2_planes[b], 0, 3, nc.scalar.copy)
+            if last and t == 3:
+                interleave(x1_grouped[b], x1_planes[b], 2, 4, nc.vector.tensor_copy)
+
+        def quantise_x(grouped, name):
+            codes = keep.tile([P, PAIRS], U32, name=name + "_codes", align_bytes=ALIGN)
+            scales = keep.tile([P, PAIRS], U8, name=name + "_sc", align_bytes=ALIGN)
+            nc.vector.quantize_mx(out=codes[:].bitcast(FP8X4), scales=scales[:], in_=grouped[:])
+            return codes, scales
+
+        e_ps = []
+
+        def second_stage(b):
+            last = b == H_PASSES - 1
+            x1_codes, x1_sc = quantise_x(x1_grouped[b], "x1_%d" % b)
+            x2_codes, x2_sc = quantise_x(x2_grouped[b], "x2_%d" % b)
+            for mt in range(PAIRS // P):
+                if b == 0:
+                    e_ps.append(psum.tile([P, PAIRS], F32, name="e_ps%d" % mt, tag="shared_bank"))
+                nc.tensor.matmul_mx(
+                    out=e_ps[mt][:],
+                    lhsT=x1_codes[:, mt * P : (mt + 1) * P].bitcast(FP8X4),
+                    lhsT_scale=x1_sc[:, mt * P : (mt + 1) * P],
+                    rhs=x2_codes[:].bitcast(FP8X4),
+                    rhs_scale=x2_sc[:],
+                    start=(b == 0),
+                    stop=last,
+                )
+
+        w1_late = {}
+        cosine(0)
+        cosine(1)
+        for i in range(ROW_TILES):
+            if i < K_PASSES:
+                w1_late[i] = round_w1(i, 1, nc.scalar.copy)
+            combine(i)
+            if i == 1:
+                for a in range(K_PASSES):
+                    quantise_w1(a, 1, w1_late[a])
+            if i + 2 < ROW_TILES:
+                cosine(i + 2)
+            pick(i)
+            if i % PACK == PACK - 1:
+                second_stage(i // PACK)
+
+        for mt in range(PAIRS // P):
+            result = ring.tile([P, PAIRS], F32, name="result", bufs=4)
+            nc.vector.tensor_tensor(result[:], e_ps[mt][:], shared_sb[:, mt, :], ALU.mult)
+            nc.sync.dma_start(out[mt * P : (mt + 1) * P, :], result[:])

@@ -30,7 +30,9 @@ RUN = 8
 GROUPS = P // RUN
 ALIGN = 64
 TURN = 1.0 / (2.0 * math.pi)
-VECTOR_REDUCED = 3
+VECTOR_REDUCED = 8
+GPSIMD_TILES = 7
+EARLY_TANH = 4
 
 
 def tile_list_softplay_pair_grid_kernel(
@@ -47,20 +49,24 @@ def tile_list_softplay_pair_grid_kernel(
         pos1_sb = lists.tile([P, PAIRS // 16], U16, name="pos1_sb")
         pos2_sb = lists.tile([P, PAIRS // 16], U16, name="pos2_sb")
         nc.sync.dma_start(offs_sb[:], offs)
-        nc.sync.dma_start(pos1_sb[:], pos1)
-        nc.sync.dma_start(pos2_sb[:], pos2)
 
         def staging(slot, shape, dtype, name):
             return keep.tile(shape, dtype, name=name, tag="staging%d" % slot, align_bytes=ALIGN)
 
-        tab_sc = staging(1, [P, K_PASSES, T], U8, "tab_sc")
-        nc.vector.memset(tab_sc[:].rearrange("p a t -> p (a t)").bitcast(I32), 0)
+        tab_sc = staging(1, [P, T], U8, "tab_sc")
+        nc.sync.dma_start(tab_sc[0:32, :].bitcast(I32), tab_scales.rearrange("a q t -> (a q) t").bitcast(I32))
         w4_sc_raw = keep.tile([P, K_PASSES, H], U8, name="w4_sc_raw", align_bytes=ALIGN)
         nc.vector.memset(w4_sc_raw[:].rearrange("p a c -> p (a c)").bitcast(I32), 0)
         vec_rows = keep.tile([P, H_PASSES * P], F32, name="vec_rows")
         nc.vector.memset(vec_rows[:], 0.0)
+        unread = keep.tile([P, 1], F32, name="unread")
+        nc.scalar.activation(unread[:], vec_rows[:, 0:1], ACT.Silu)
+        nc.vector.memset(tab_sc[32:64, :].bitcast(I32), 0)
+        nc.vector.memset(tab_sc[64:128, :].bitcast(I32), 0)
+        v_sc = keep.tile([P, K_PASSES, S], U8, name="v_sc", align_bytes=ALIGN)
+        nc.vector.memset(v_sc[:].rearrange("p a s -> p (a s)").bitcast(I32), 0)
 
-        w4_raw = staging(0, [P, K_PASSES, H // 2], I32, "w4_raw")
+        w4_raw = keep.tile([P, K_PASSES, H // 2], I32, name="w4_raw")
         nc.sync.dma_start(w4_raw[:], w4_words.rearrange("a p n -> p a n").bitcast(I32))
         tab = {}
 
@@ -69,16 +75,29 @@ def tile_list_softplay_pair_grid_kernel(
             nc.sync.dma_start(tab[a][:], tab_words[a].rearrange("p t i -> p (t i)").bitcast(I32))
 
         load_table(0, 2)
+        nc.sync.dma_start(pos1_sb[:], pos1)
+        nc.sync.dma_start(pos2_sb[:], pos2)
+        load_table(1, 0)
         for q in range(4):
-            nc.scalar.dma_start(
-                tab_sc[32 * q : 32 * q + 4, :, :].bitcast(I32),
-                tab_scales[:, 4 * q : 4 * q + 4, :].rearrange("a r t -> r a t").bitcast(I32),
-            )
-        for q in range(4):
-            (nc.gpsimd if q < 2 else nc.scalar).dma_start(
+            nc.gpsimd.dma_start(
                 w4_sc_raw[32 * q : 32 * q + 4, :, :].bitcast(I32),
                 w4_scales[:, 4 * q : 4 * q + 4, :].rearrange("a r c -> r a c").bitcast(I32),
             )
+        w4_codes = keep.tile([P, K_PASSES, H // 2], I32, name="w4_codes", align_bytes=ALIGN)
+        nc.vector.tensor_copy(
+            w4_codes[:].rearrange("p a (b t g w) -> p (a b) t g w", b=H_PASSES, t=PACK, g=GROUPS),
+            w4_raw[:].rearrange("p a (b g t w) -> p (a b) t g w", b=H_PASSES, t=PACK, g=GROUPS),
+        )
+
+        picked_sc = keep.tile([P, S], U8, name="picked_sc", align_bytes=ALIGN)
+        nc.vector.tensor_copy(picked_sc[:], tab_sc[:].indirect(offs_sb[:]))
+        for a in range(K_PASSES):
+            for q in range(4):
+                (nc.scalar if a == 0 else nc.gpsimd).dma_start(
+                    v_sc[32 * q : 32 * q + 4, a, :].bitcast(I32),
+                    picked_sc[16 * a + 4 * q : 16 * a + 4 * q + 4, :].bitcast(I32),
+                )
+
         for v, vec in enumerate((gain, worth)):
             nc.gpsimd.dma_start(
                 vec_rows[PACK * v : PACK * (v + 1), :].rearrange("t (g e) -> t g e", e=RUN),
@@ -86,18 +105,6 @@ def tile_list_softplay_pair_grid_kernel(
             )
         ident = keep.tile([P, P], F32, name="ident")
         make_identity(nc, ident[:])
-
-        w4_codes = keep.tile([P, K_PASSES, H // 2], I32, name="w4_codes", align_bytes=ALIGN)
-        nc.vector.tensor_copy(
-            w4_codes[:].rearrange("p a (b t g w) -> p (a b) t g w", b=H_PASSES, t=PACK, g=GROUPS),
-            w4_raw[:].rearrange("p a (b g t w) -> p (a b) t g w", b=H_PASSES, t=PACK, g=GROUPS),
-        )
-
-        load_table(1, 0)
-
-        v_sc = [keep.tile([P, S], U8, name="v_sc%d" % a, align_bytes=ALIGN) for a in range(K_PASSES)]
-        for a in range(K_PASSES):
-            nc.vector.tensor_copy(v_sc[a][:], tab_sc[:, a, :].indirect(offs_sb[:]))
 
         w4_sc = keep.tile([P, K_PASSES, H], U8, name="w4_sc", align_bytes=ALIGN)
         nc.vector.tensor_copy(
@@ -127,23 +134,23 @@ def tile_list_softplay_pair_grid_kernel(
         w1_codes = {}
         w1_sc = {}
 
-        def round_w1(a, b, copy):
-            grouped = ring.tile([P, PASS * PACK], BF16, name="w1_grouped", align_bytes=ALIGN)
+        def round_w1(a, b, u, copy):
+            grouped = ring.tile([P, 2 * P * PACK], BF16, name="w1_grouped", align_bytes=ALIGN, bufs=4)
             copy(
-                grouped[:].rearrange("p (t g e j) -> p t g e j", t=PACK, g=GROUPS, e=RUN),
-                w1_raw[a, b][:].rearrange("p j (g t e) -> p t g e j", t=PACK, e=RUN),
+                grouped[:].rearrange("p (t g e j) -> p t g e j", t=2, g=GROUPS, e=RUN),
+                w1_raw[a, b][:].rearrange("p j (g t e) -> p t g e j", t=PACK, e=RUN)[:, 2 * u : 2 * u + 2],
             )
             return grouped
 
-        def quantise_w1(a, b, grouped):
-            w1_codes[a, b] = keep.tile([P, PASS], U32, name="w1_codes%d%d" % (a, b), align_bytes=ALIGN)
-            w1_sc[a, b] = keep.tile([P, PASS], U8, name="w1_sc%d%d" % (a, b), align_bytes=ALIGN)
-            nc.vector.quantize_mx(out=w1_codes[a, b][:].bitcast(FP8X4), scales=w1_sc[a, b][:], in_=grouped[:])
+        def quantise_w1(a, b, u, grouped):
+            w1_codes[a, b, u] = keep.tile([P, 2 * P], U32, name="w1_codes%d%d%d" % (a, b, u), align_bytes=ALIGN)
+            w1_sc[a, b, u] = keep.tile([P, 2 * P], U8, name="w1_sc%d%d%d" % (a, b, u), align_bytes=ALIGN)
+            nc.vector.quantize_mx(out=w1_codes[a, b, u][:].bitcast(FP8X4), scales=w1_sc[a, b, u][:], in_=grouped[:])
 
-        tanh_b = []
-        for i in range(ROW_TILES):
-            th = keep.tile([P, S], F32, name="tanh_b%d" % i)
-            tanh_b.append(th)
+        tanh_b = {}
+
+        def tanh_product(i):
+            tanh_b[i] = keep.tile([P, S], F32, name="tanh_b%d" % i)
             for hf in range(HALVES):
                 acc = psum.tile([P, BANK], F32, name="b_ps", tag="shared_bank")
                 for a in range(K_PASSES):
@@ -152,20 +159,19 @@ def tile_list_softplay_pair_grid_kernel(
                         lhsT=w4_codes[:, a, i * P // 2 : (i + 1) * P // 2].bitcast(U8).bitcast(FP4X4),
                         lhsT_scale=w4_sc[:, a, i * P : (i + 1) * P],
                         rhs=v_codes[a, hf][:].bitcast(FP8X4),
-                        rhs_scale=v_sc[a][:, hf * BANK : (hf + 1) * BANK],
+                        rhs_scale=v_sc[:, a, hf * BANK : (hf + 1) * BANK],
                         start=(a == 0),
                         stop=(a == K_PASSES - 1),
                     )
-                nc.scalar.activation(th[:, hf * BANK : (hf + 1) * BANK], acc[:], ACT.Tanh)
+                nc.scalar.activation(tanh_b[i][:, hf * BANK : (hf + 1) * BANK], acc[:], ACT.Tanh)
 
-        vec_ps = psum.tile([P, H_PASSES, P], F32, name="vec_ps", tag="shared_bank")
-        for b in range(H_PASSES):
-            nc.tensor.transpose(vec_ps[:, b, :], vec_rows[:, b * P : (b + 1) * P], ident[:])
-        vecs = keep.tile([P, H_PASSES, 2 * PACK], F32, name="vecs")
-        nc.vector.tensor_copy(vecs[:], vec_ps[:, :, 0 : 2 * PACK])
+        for i in range(EARLY_TANH):
+            tanh_product(i)
 
         for a in range(K_PASSES):
-            quantise_w1(a, 0, round_w1(a, 0, nc.vector.tensor_copy))
+            halves = [round_w1(a, 0, u, nc.vector.tensor_copy) for u in range(2)]
+            for u in range(2):
+                quantise_w1(a, 0, u, halves[u])
 
         load_w1(0, 1, 1)
         shared_sb = staging(2, [P, PAIRS // P, PAIRS], F32, "shared_sb")
@@ -184,10 +190,10 @@ def tile_list_softplay_pair_grid_kernel(
                 for a in range(K_PASSES):
                     nc.tensor.matmul_mx(
                         out=acc[:],
-                        lhsT=w1_codes[a, b][:, t * P : (t + 1) * P].bitcast(FP8X4),
-                        lhsT_scale=w1_sc[a, b][:, t * P : (t + 1) * P],
+                        lhsT=w1_codes[a, b, t // 2][:, t % 2 * P : (t % 2 + 1) * P].bitcast(FP8X4),
+                        lhsT_scale=w1_sc[a, b, t // 2][:, t % 2 * P : (t % 2 + 1) * P],
                         rhs=v_codes[a, hf][:].bitcast(FP8X4),
-                        rhs_scale=v_sc[a][:, hf * BANK : (hf + 1) * BANK],
+                        rhs_scale=v_sc[:, a, hf * BANK : (hf + 1) * BANK],
                         start=(a == 0),
                         stop=(a == K_PASSES - 1),
                     )
@@ -215,9 +221,12 @@ def tile_list_softplay_pair_grid_kernel(
         def combine(i):
             b, t = divmod(i, PACK)
             h[i] = ring.tile([P, S], F32, name="h")
-            nc.vector.scalar_tensor_tensor(
-                h[i][:], cos_a[i][:], vecs[:, b, t : t + 1], tanh_b[i][:], ALU.mult, ALU.mult
-            )
+            if i < GPSIMD_TILES:
+                nc.gpsimd.tensor_tensor(h[i][:], cos_a[i][:], tanh_b[i][:], ALU.mult)
+            else:
+                nc.vector.scalar_tensor_tensor(
+                    h[i][:], cos_a[i][:], vecs[:, b, t : t + 1], tanh_b[i][:], ALU.mult, ALU.mult
+                )
 
         x1_planes = {}
         x2_planes = {}
@@ -240,13 +249,20 @@ def tile_list_softplay_pair_grid_kernel(
                 x2_grouped[b] = ring.tile([P, PAIRS * PACK], BF16, name="x2_grouped", align_bytes=ALIGN, bufs=1)
             picked = ring.tile([P, PAIRS], F32, name="picked")
             nc.vector.tensor_copy(picked[:], h[i][:].indirect(pos2_sb[:]))
-            nc.vector.tensor_copy(x1_planes[b][:, t, :], h[i][:].indirect(pos1_sb[:]))
-            nc.scalar.activation(picked[:], picked[:], ACT.Abs)
+            if i < GPSIMD_TILES:
+                picked1 = ring.tile([P, PAIRS], F32, name="picked1")
+                nc.vector.tensor_copy(picked1[:], h[i][:].indirect(pos1_sb[:]))
+                nc.scalar.activation(picked[:], picked[:], ACT.Abs, scale=vecs[:, b, t : t + 1])
+            else:
+                nc.vector.tensor_copy(x1_planes[b][:, t, :], h[i][:].indirect(pos1_sb[:]))
+                nc.scalar.activation(picked[:], picked[:], ACT.Abs)
             if last and t == PACK - 1:
                 x2_out = x2_grouped[b][:].rearrange("p (c t) -> p t c", t=PACK)[:, t, :]
             else:
                 x2_out = x2_planes[b][:, t, :]
             nc.scalar.activation(x2_out, picked[:], ACT.Copy, scale=vecs[:, b, PACK + t : PACK + t + 1])
+            if i < GPSIMD_TILES:
+                nc.scalar.activation(x1_planes[b][:, t, :], picked1[:], ACT.Copy, scale=vecs[:, b, t : t + 1])
             if not last and t == PACK - 1:
                 interleave(x2_grouped[b], x2_planes[b], 0, PACK, nc.scalar.copy)
                 interleave(x1_grouped[b], x1_planes[b], 0, PACK, nc.scalar.copy)
@@ -282,19 +298,28 @@ def tile_list_softplay_pair_grid_kernel(
                     stop=last,
                 )
 
-        w1_late = {}
         cosine(0)
         cosine(1)
+        vec_ps = psum.tile([P, H_PASSES, P], F32, name="vec_ps", tag="a_ps")
+        for b in range(H_PASSES):
+            nc.tensor.transpose(vec_ps[:, b, :], vec_rows[:, b * P : (b + 1) * P], ident[:])
+        vecs = keep.tile([P, H_PASSES, 2 * PACK], F32, name="vecs")
+        nc.vector.tensor_copy(vecs[:], vec_ps[:, :, 0 : 2 * PACK])
+
+        combine(0)
+        for i in range(EARLY_TANH, ROW_TILES):
+            tanh_product(i)
         for i in range(ROW_TILES):
-            if i < K_PASSES:
-                w1_late[i] = round_w1(i, 1, nc.scalar.copy)
-            combine(i)
-            if i == 1:
-                for a in range(K_PASSES):
-                    quantise_w1(a, 1, w1_late[a])
+            if i < 2:
+                late = [round_w1(a, 1, i, nc.scalar.copy) for a in range(K_PASSES)]
             if i + 2 < ROW_TILES:
                 cosine(i + 2)
+            if i + 1 < ROW_TILES:
+                combine(i + 1)
             pick(i)
+            if i < 2:
+                for a in range(K_PASSES):
+                    quantise_w1(a, 1, i, late[a])
             if i % PACK == PACK - 1:
                 second_stage(i // PACK)
 

@@ -142,6 +142,19 @@ def tile_list_softplay_pair_grid_kernel(
             )
             return grouped
 
+        def round_w1_gpsimd(a, b, u):
+            grouped = ring.tile([P, 2 * P * PACK], BF16, name="w1_grouped", align_bytes=ALIGN, bufs=4)
+            for t in range(2):
+                nc.gpsimd.tensor_scalar(
+                    grouped[:].rearrange("p (t g e j) -> p t g e j", t=2, g=GROUPS, e=RUN)[:, t],
+                    w1_raw[a, b][:].rearrange("p j (g t e) -> p t g e j", t=PACK, e=RUN)[:, 2 * u + t],
+                    1.0,
+                    0.0,
+                    ALU.mult,
+                    ALU.add,
+                )
+            return grouped
+
         def quantise_w1(a, b, u, grouped):
             w1_codes[a, b, u] = keep.tile([P, 2 * P], U32, name="w1_codes%d%d%d" % (a, b, u), align_bytes=ALIGN)
             w1_sc[a, b, u] = keep.tile([P, 2 * P], U8, name="w1_sc%d%d%d" % (a, b, u), align_bytes=ALIGN)
@@ -169,7 +182,7 @@ def tile_list_softplay_pair_grid_kernel(
             tanh_product(i)
 
         for a in range(K_PASSES):
-            halves = [round_w1(a, 0, u, nc.vector.tensor_copy) for u in range(2)]
+            halves = [round_w1(a, 0, u, copy) for u, copy in enumerate((nc.vector.tensor_copy, nc.scalar.copy))]
             for u in range(2):
                 quantise_w1(a, 0, u, halves[u])
 
@@ -256,11 +269,7 @@ def tile_list_softplay_pair_grid_kernel(
             else:
                 nc.vector.tensor_copy(x1_planes[b][:, t, :], h[i][:].indirect(pos1_sb[:]))
                 nc.scalar.activation(picked[:], picked[:], ACT.Abs)
-            if last and t == PACK - 1:
-                x2_out = x2_grouped[b][:].rearrange("p (c t) -> p t c", t=PACK)[:, t, :]
-            else:
-                x2_out = x2_planes[b][:, t, :]
-            nc.scalar.activation(x2_out, picked[:], ACT.Copy, scale=vecs[:, b, PACK + t : PACK + t + 1])
+            nc.scalar.activation(x2_planes[b][:, t, :], picked[:], ACT.Copy, scale=vecs[:, b, PACK + t : PACK + t + 1])
             if i < GPSIMD_TILES:
                 nc.scalar.activation(x1_planes[b][:, t, :], picked1[:], ACT.Copy, scale=vecs[:, b, t : t + 1])
             if not last and t == PACK - 1:
@@ -268,10 +277,10 @@ def tile_list_softplay_pair_grid_kernel(
                 interleave(x1_grouped[b], x1_planes[b], 0, PACK, nc.scalar.copy)
             if last and t == 1:
                 interleave(x1_grouped[b], x1_planes[b], 0, 2, nc.scalar.copy)
-            if last and t == 2:
-                interleave(x2_grouped[b], x2_planes[b], 0, 3, nc.scalar.copy)
+                interleave(x2_grouped[b], x2_planes[b], 0, 2, nc.scalar.copy)
             if last and t == 3:
                 interleave(x1_grouped[b], x1_planes[b], 2, 4, nc.vector.tensor_copy)
+                interleave(x2_grouped[b], x2_planes[b], 2, 4, nc.vector.tensor_copy)
 
         def quantise_x(grouped, name):
             codes = keep.tile([P, PAIRS], U32, name=name + "_codes", align_bytes=ALIGN)
@@ -306,12 +315,11 @@ def tile_list_softplay_pair_grid_kernel(
         vecs = keep.tile([P, H_PASSES, 2 * PACK], F32, name="vecs")
         nc.vector.tensor_copy(vecs[:], vec_ps[:, :, 0 : 2 * PACK])
 
+        late = {(a, u): round_w1_gpsimd(a, 1, u) for a in (1, 0) for u in range(2)}
         combine(0)
         for i in range(EARLY_TANH, ROW_TILES):
             tanh_product(i)
         for i in range(ROW_TILES):
-            if i < 2:
-                late = [round_w1(a, 1, i, nc.scalar.copy) for a in range(K_PASSES)]
             if i + 2 < ROW_TILES:
                 cosine(i + 2)
             if i + 1 < ROW_TILES:
@@ -319,7 +327,7 @@ def tile_list_softplay_pair_grid_kernel(
             pick(i)
             if i < 2:
                 for a in range(K_PASSES):
-                    quantise_w1(a, 1, i, late[a])
+                    quantise_w1(a, 1, i, late[a, i])
             if i % PACK == PACK - 1:
                 second_stage(i // PACK)
 

@@ -246,10 +246,12 @@ def tile_list_softplay_pair_grid_kernel(
         x1_grouped = {}
         x2_grouped = {}
 
-        def interleave(grouped, planes, first, end, copy):
+        def interleave(grouped, planes, first, end, copy, cols=slice(0, PAIRS)):
             copy(
-                grouped[:].rearrange("p (c i t) -> p c t i", i=4, t=PACK)[:, :, first:end, :],
-                planes[:, first:end, :].rearrange("p t (c i) -> p c t i", i=4),
+                grouped[:, cols.start * PACK : cols.stop * PACK].rearrange("p (c i t) -> p c t i", i=4, t=PACK)[
+                    :, :, first:end, :
+                ],
+                planes[:, first:end, cols].rearrange("p t (c i) -> p c t i", i=4),
             )
 
         def pick(i):
@@ -258,8 +260,8 @@ def tile_list_softplay_pair_grid_kernel(
             if t == 0:
                 x1_planes[b] = ring.tile([P, PACK, PAIRS], BF16, name="x1_planes")
                 x2_planes[b] = ring.tile([P, PACK, PAIRS], BF16, name="x2_planes")
-                x1_grouped[b] = ring.tile([P, PAIRS * PACK], BF16, name="x1_grouped", align_bytes=ALIGN, bufs=1)
-                x2_grouped[b] = ring.tile([P, PAIRS * PACK], BF16, name="x2_grouped", align_bytes=ALIGN, bufs=1)
+                x1_grouped[b] = ring.tile([P, PAIRS * PACK], BF16, name="x1_grouped", align_bytes=ALIGN)
+                x2_grouped[b] = ring.tile([P, PAIRS * PACK], BF16, name="x2_grouped", align_bytes=ALIGN)
             picked = ring.tile([P, PAIRS], F32, name="picked")
             nc.vector.tensor_copy(picked[:], h[i][:].indirect(pos2_sb[:]))
             if i < GPSIMD_TILES:
@@ -272,28 +274,38 @@ def tile_list_softplay_pair_grid_kernel(
             nc.scalar.activation(x2_planes[b][:, t, :], picked[:], ACT.Copy, scale=vecs[:, b, PACK + t : PACK + t + 1])
             if i < GPSIMD_TILES:
                 nc.scalar.activation(x1_planes[b][:, t, :], picked1[:], ACT.Copy, scale=vecs[:, b, t : t + 1])
-            if not last and t == PACK - 1:
-                interleave(x2_grouped[b], x2_planes[b], 0, PACK, nc.scalar.copy)
-                interleave(x1_grouped[b], x1_planes[b], 0, PACK, nc.scalar.copy)
             if last and t == 1:
-                interleave(x1_grouped[b], x1_planes[b], 0, 2, nc.scalar.copy)
                 interleave(x2_grouped[b], x2_planes[b], 0, 2, nc.scalar.copy)
-            if last and t == 3:
-                interleave(x1_grouped[b], x1_planes[b], 2, 4, nc.vector.tensor_copy)
-                interleave(x2_grouped[b], x2_planes[b], 2, 4, nc.vector.tensor_copy)
 
-        def quantise_x(grouped, name):
+        def mx_tiles(name):
             codes = keep.tile([P, PAIRS], U32, name=name + "_codes", align_bytes=ALIGN)
             scales = keep.tile([P, PAIRS], U8, name=name + "_sc", align_bytes=ALIGN)
-            nc.vector.quantize_mx(out=codes[:].bitcast(FP8X4), scales=scales[:], in_=grouped[:])
             return codes, scales
+
+        def quantise_x(grouped, codes, scales, cols=slice(0, PAIRS)):
+            nc.vector.quantize_mx(
+                out=codes[:, cols].bitcast(FP8X4),
+                scales=scales[:, cols],
+                in_=grouped[:, cols.start * PACK : cols.stop * PACK],
+            )
 
         e_ps = []
 
         def second_stage(b):
             last = b == H_PASSES - 1
-            x1_codes, x1_sc = quantise_x(x1_grouped[b], "x1_%d" % b)
-            x2_codes, x2_sc = quantise_x(x2_grouped[b], "x2_%d" % b)
+            x1_codes, x1_sc = mx_tiles("x1_%d" % b)
+            x2_codes, x2_sc = mx_tiles("x2_%d" % b)
+            if last:
+                low, high = slice(0, PAIRS // 2), slice(PAIRS // 2, PAIRS)
+                interleave(x2_grouped[b], x2_planes[b], 2, 4, nc.vector.tensor_copy)
+                interleave(x1_grouped[b], x1_planes[b], 0, 4, nc.vector.tensor_copy, low)
+                quantise_x(x2_grouped[b], x2_codes, x2_sc)
+                quantise_x(x1_grouped[b], x1_codes, x1_sc, low)
+                interleave(x1_grouped[b], x1_planes[b], 0, 4, nc.vector.tensor_copy, high)
+                quantise_x(x1_grouped[b], x1_codes, x1_sc, high)
+            else:
+                quantise_x(x2_grouped[b], x2_codes, x2_sc)
+                quantise_x(x1_grouped[b], x1_codes, x1_sc)
             for mt in range(PAIRS // P):
                 if b == 0:
                     e_ps.append(psum.tile([P, PAIRS], F32, name="e_ps%d" % mt, tag="shared_bank"))
@@ -315,21 +327,28 @@ def tile_list_softplay_pair_grid_kernel(
         vecs = keep.tile([P, H_PASSES, 2 * PACK], F32, name="vecs")
         nc.vector.tensor_copy(vecs[:], vec_ps[:, :, 0 : 2 * PACK])
 
-        late = {(a, u): round_w1_gpsimd(a, 1, u) for a in (1, 0) for u in range(2)}
+        late = {(a, 0): round_w1_gpsimd(a, 1, 0) for a in (1, 0)}
         combine(0)
-        for i in range(EARLY_TANH, ROW_TILES):
-            tanh_product(i)
         for i in range(ROW_TILES):
             if i + 2 < ROW_TILES:
                 cosine(i + 2)
             if i + 1 < ROW_TILES:
                 combine(i + 1)
+            if i == PACK:
+                interleave(x2_grouped[0], x2_planes[0], 0, PACK, nc.scalar.copy)
+            if i == PACK + 1:
+                interleave(x1_grouped[0], x1_planes[0], 0, PACK, nc.scalar.copy)
             pick(i)
-            if i < 2:
+            if EARLY_TANH + i < ROW_TILES:
+                tanh_product(EARLY_TANH + i)
+            if i in (1, 2):
+                late[i - 1, 1] = round_w1(i - 1, 1, 1, nc.scalar.copy)
+            if i in (0, 3):
                 for a in range(K_PASSES):
-                    quantise_w1(a, 1, i, late[a, i])
-            if i % PACK == PACK - 1:
-                second_stage(i // PACK)
+                    quantise_w1(a, 1, i // 3, late[a, i // 3])
+            if i == PACK + 1:
+                second_stage(0)
+        second_stage(1)
 
         for mt in range(PAIRS // P):
             result = ring.tile([P, PAIRS], F32, name="result", bufs=4)

import math
from contextlib import ExitStack

import concourse.mybir as mybir
from concourse.masks import make_identity

K, T, S, H, PAIRS = 1024, 4096, 1024, 1024, 512
FLOPS = 2 * (2 * K * H * S + H * PAIRS * PAIRS)

F32 = mybir.dt.float32
BF16 = mybir.dt.bfloat16
I32 = mybir.dt.int32
U32 = mybir.dt.uint32
U16 = mybir.dt.uint16
U8 = mybir.dt.uint8
FP8X4 = mybir.dt.float8_e4m3fn_x4
FP4X4 = mybir.dt.float4_e2m1fn_x4
ALU = mybir.AluOpType
ACT = mybir.ActivationFunctionType

P = 128
PACK = 4
PASS = P * PACK
K_PASSES = K // PASS
H_PASSES = H // PASS
ROW_TILES = H // P
BANK = 512
HALVES = S // BANK
RUN = 8
GROUPS = P // RUN
ALIGN = 64
TURN = 1.0 / (2.0 * math.pi)
VECTOR_REDUCED = 8
GPSIMD_TILES = 7
EARLY_TANH = 4


def tile_list_softplay_pair_grid_kernel(
    tc, tab_words, tab_scales, w1, w4_words, w4_scales, gain, worth, shared, offs, pos1, pos2, out
):
    nc = tc.nc
    with ExitStack() as ctx:
        lists = ctx.enter_context(tc.tile_pool(name="lists", bufs=1))
        keep = ctx.enter_context(tc.tile_pool(name="keep", bufs=1))
        ring = ctx.enter_context(tc.tile_pool(name="ring", bufs=2))
        psum = ctx.enter_context(tc.psum_pool(name="psum", bufs=4))

        offs_sb = lists.tile([P, S // 16], U16, name="offs_sb")
        pos1_sb = lists.tile([P, PAIRS // 16], U16, name="pos1_sb")
        pos2_sb = lists.tile([P, PAIRS // 16], U16, name="pos2_sb")
        nc.sync.dma_start(offs_sb[:], offs)

        def staging(slot, shape, dtype, name):
            return keep.tile(shape, dtype, name=name, tag="staging%d" % slot, align_bytes=ALIGN)

        tab_sc = staging(1, [P, T], U8, "tab_sc")
        nc.sync.dma_start(tab_sc[0:32, :].bitcast(I32), tab_scales.rearrange("a q t -> (a q) t").bitcast(I32))
        w4_sc_raw = keep.tile([P, K_PASSES, H], U8, name="w4_sc_raw", align_bytes=ALIGN)
        nc.vector.memset(w4_sc_raw[:].rearrange("p a c -> p (a c)").bitcast(I32), 0)
        vec_rows = keep.tile([P, H_PASSES * P], F32, name="vec_rows")
        nc.vector.memset(vec_rows[:], 0.0)
        unread = keep.tile([P, 1], F32, name="unread")
        nc.scalar.activation(unread[:], vec_rows[:, 0:1], ACT.Silu)
        nc.vector.memset(tab_sc[32:64, :].bitcast(I32), 0)
        nc.vector.memset(tab_sc[64:128, :].bitcast(I32), 0)
        v_sc = keep.tile([P, K_PASSES, S], U8, name="v_sc", align_bytes=ALIGN)
        nc.vector.memset(v_sc[:].rearrange("p a s -> p (a s)").bitcast(I32), 0)

        w4_raw = keep.tile([P, K_PASSES, H // 2], I32, name="w4_raw")
        nc.sync.dma_start(w4_raw[:], w4_words.rearrange("a p n -> p a n").bitcast(I32))
        tab = {}

        def load_table(a, slot):
            tab[a] = staging(slot, [P, T], I32, "tab%d" % a)
            nc.sync.dma_start(tab[a][:], tab_words[a].rearrange("p t i -> p (t i)").bitcast(I32))

        load_table(0, 2)
        nc.sync.dma_start(pos1_sb[:], pos1)
        nc.sync.dma_start(pos2_sb[:], pos2)
        load_table(1, 0)
        for q in range(4):
            nc.gpsimd.dma_start(
                w4_sc_raw[32 * q : 32 * q + 4, :, :].bitcast(I32),
                w4_scales[:, 4 * q : 4 * q + 4, :].rearrange("a r c -> r a c").bitcast(I32),
            )
        w4_codes = keep.tile([P, K_PASSES, H // 2], I32, name="w4_codes", align_bytes=ALIGN)
        nc.vector.tensor_copy(
            w4_codes[:].rearrange("p a (b t g w) -> p (a b) t g w", b=H_PASSES, t=PACK, g=GROUPS),
            w4_raw[:].rearrange("p a (b g t w) -> p (a b) t g w", b=H_PASSES, t=PACK, g=GROUPS),
        )

        picked_sc = keep.tile([P, S], U8, name="picked_sc", align_bytes=ALIGN)
        nc.vector.tensor_copy(picked_sc[:], tab_sc[:].indirect(offs_sb[:]))
        for a in range(K_PASSES):
            for q in range(4):
                (nc.scalar if a == 0 else nc.gpsimd).dma_start(
                    v_sc[32 * q : 32 * q + 4, a, :].bitcast(I32),
                    picked_sc[16 * a + 4 * q : 16 * a + 4 * q + 4, :].bitcast(I32),
                )

        for v, vec in enumerate((gain, worth)):
            nc.gpsimd.dma_start(
                vec_rows[PACK * v : PACK * (v + 1), :].rearrange("t (g e) -> t g e", e=RUN),
                vec.rearrange("(g t e) -> t g e", t=PACK, e=RUN),
            )
        ident = keep.tile([P, P], F32, name="ident")
        make_identity(nc, ident[:])

        w4_sc = keep.tile([P, K_PASSES, H], U8, name="w4_sc", align_bytes=ALIGN)
        nc.vector.tensor_copy(
            w4_sc[:].bitcast(I32).rearrange("p a (b t g w) -> p (a b) t g w", b=H_PASSES, t=PACK, g=GROUPS),
            w4_sc_raw[:].bitcast(I32).rearrange("p a (b g t w) -> p (a b) t g w", b=H_PASSES, t=PACK, g=GROUPS),
        )

        v_codes = {}
        for a in range(K_PASSES):
            for hf in range(HALVES):
                v_codes[a, hf] = keep.tile([P, BANK], U32, name="v_codes%d%d" % (a, hf), align_bytes=ALIGN)
                cols = slice(hf * BANK // 16, (hf + 1) * BANK // 16)
                nc.vector.tensor_copy(v_codes[a, hf][:], tab[a][:].bitcast(U32).indirect(offs_sb[:, cols]))

        w1_raw = {}

        def load_w1(a, b, slot):
            w1_raw[a, b] = staging(slot, [P, PACK, PASS], F32, "w1_raw%d%d" % (a, b))
            nc.sync.dma_start(
                w1_raw[a, b][:],
                w1[a * PASS : (a + 1) * PASS, b * PASS : (b + 1) * PASS].rearrange("(p j) c -> p j c", j=PACK),
            )

        load_w1(0, 0, 1)
        load_w1(1, 0, 2)
        load_w1(1, 1, 0)
        w1_codes = {}
        w1_sc = {}

        def round_w1(a, b, u, copy):
            grouped = ring.tile([P, 2 * P * PACK], BF16, name="w1_grouped", align_bytes=ALIGN, bufs=4)
            copy(
                grouped[:].rearrange("p (t g e j) -> p t g e j", t=2, g=GROUPS, e=RUN),
                w1_raw[a, b][:].rearrange("p j (g t e) -> p t g e j", t=PACK, e=RUN)[:, 2 * u : 2 * u + 2],
            )
            return grouped

        def round_w1_gpsimd(a, b, u):
            grouped = ring.tile([P, 2 * P * PACK], BF16, name="w1_grouped", align_bytes=ALIGN, bufs=4)
            for t in range(2):
                nc.gpsimd.tensor_scalar(
                    grouped[:].rearrange("p (t g e j) -> p t g e j", t=2, g=GROUPS, e=RUN)[:, t],
                    w1_raw[a, b][:].rearrange("p j (g t e) -> p t g e j", t=PACK, e=RUN)[:, 2 * u + t],
                    1.0,
                    0.0,
                    ALU.mult,
                    ALU.add,
                )
            return grouped

        def quantise_w1(a, b, u, grouped):
            w1_codes[a, b, u] = keep.tile([P, 2 * P], U32, name="w1_codes%d%d%d" % (a, b, u), align_bytes=ALIGN)
            w1_sc[a, b, u] = keep.tile([P, 2 * P], U8, name="w1_sc%d%d%d" % (a, b, u), align_bytes=ALIGN)
            nc.vector.quantize_mx(out=w1_codes[a, b, u][:].bitcast(FP8X4), scales=w1_sc[a, b, u][:], in_=grouped[:])

        tanh_b = {}

        def tanh_product(i):
            tanh_b[i] = keep.tile([P, S], F32, name="tanh_b%d" % i)
            for hf in range(HALVES):
                acc = psum.tile([P, BANK], F32, name="b_ps", tag="shared_bank")
                for a in range(K_PASSES):
                    nc.tensor.matmul_mx(
                        out=acc[:],
                        lhsT=w4_codes[:, a, i * P // 2 : (i + 1) * P // 2].bitcast(U8).bitcast(FP4X4),
                        lhsT_scale=w4_sc[:, a, i * P : (i + 1) * P],
                        rhs=v_codes[a, hf][:].bitcast(FP8X4),
                        rhs_scale=v_sc[:, a, hf * BANK : (hf + 1) * BANK],
                        start=(a == 0),
                        stop=(a == K_PASSES - 1),
                    )
                nc.scalar.activation(tanh_b[i][:, hf * BANK : (hf + 1) * BANK], acc[:], ACT.Tanh)

        for i in range(EARLY_TANH):
            tanh_product(i)

        for a in range(K_PASSES):
            halves = [round_w1(a, 0, u, copy) for u, copy in enumerate((nc.vector.tensor_copy, nc.scalar.copy))]
            for u in range(2):
                quantise_w1(a, 0, u, halves[u])

        load_w1(0, 1, 1)
        shared_sb = staging(2, [P, PAIRS // P, PAIRS], F32, "shared_sb")
        nc.sync.dma_start(shared_sb[:], shared.rearrange("(mt p) j -> p mt j", p=P))

        cos_a = {}

        def cosine(i):
            b, t = divmod(i, PACK)
            turns = ring.tile([P, S], F32, name="turns", bufs=4)
            whole = ring.tile([P, S], I32, name="whole")
            accs = []
            for hf in range(HALVES):
                acc = psum.tile([P, BANK], F32, name="a_ps")
                accs.append(acc)
                for a in range(K_PASSES):
                    nc.tensor.matmul_mx(
                        out=acc[:],
                        lhsT=w1_codes[a, b, t // 2][:, t % 2 * P : (t % 2 + 1) * P].bitcast(FP8X4),
                        lhsT_scale=w1_sc[a, b, t // 2][:, t % 2 * P : (t % 2 + 1) * P],
                        rhs=v_codes[a, hf][:].bitcast(FP8X4),
                        rhs_scale=v_sc[:, a, hf * BANK : (hf + 1) * BANK],
                        start=(a == 0),
                        stop=(a == K_PASSES - 1),
                    )
            if i < VECTOR_REDUCED:
                for hf in range(HALVES):
                    cols = slice(hf * BANK, (hf + 1) * BANK)
                    nc.vector.tensor_scalar(whole[:, cols], accs[hf][:], TURN, 0.25, ALU.mult, ALU.add)
                for hf in range(HALVES):
                    cols = slice(hf * BANK, (hf + 1) * BANK)
                    nc.vector.scalar_tensor_tensor(
                        turns[:, cols], accs[hf][:], TURN, whole[:, cols], ALU.mult, ALU.subtract
                    )
                nc.scalar.activation(turns[:], turns[:], ACT.Sin, bias=math.pi / 2.0, scale=2.0 * math.pi)
            else:
                for hf in range(HALVES):
                    cols = slice(hf * BANK, (hf + 1) * BANK)
                    nc.scalar.activation(turns[:, cols], accs[hf][:], ACT.Copy, bias=0.25, scale=TURN)
                nc.vector.tensor_copy(whole[:], turns[:])
                nc.vector.tensor_tensor(turns[:], turns[:], whole[:], ALU.subtract)
                nc.scalar.activation(turns[:], turns[:], ACT.Sin, scale=2.0 * math.pi)
            cos_a[i] = turns

        h = {}

        def combine(i):
            b, t = divmod(i, PACK)
            h[i] = ring.tile([P, S], F32, name="h")
            if i < GPSIMD_TILES:
                nc.gpsimd.tensor_tensor(h[i][:], cos_a[i][:], tanh_b[i][:], ALU.mult)
            else:
                nc.vector.scalar_tensor_tensor(
                    h[i][:], cos_a[i][:], vecs[:, b, t : t + 1], tanh_b[i][:], ALU.mult, ALU.mult
                )

        x1_planes = {}
        x2_planes = {}
        x1_grouped = {}
        x2_grouped = {}

        def interleave(grouped, planes, first, end, copy, cols=slice(0, PAIRS)):
            copy(
                grouped[:, cols.start * PACK : cols.stop * PACK].rearrange("p (c i t) -> p c t i", i=4, t=PACK)[
                    :, :, first:end, :
                ],
                planes[:, first:end, cols].rearrange("p t (c i) -> p c t i", i=4),
            )

        def pick(i):
            b, t = divmod(i, PACK)
            last = b == H_PASSES - 1
            if t == 0:
                x1_planes[b] = ring.tile([P, PACK, PAIRS], BF16, name="x1_planes")
                x2_planes[b] = ring.tile([P, PACK, PAIRS], BF16, name="x2_planes")
                x1_grouped[b] = ring.tile([P, PAIRS * PACK], BF16, name="x1_grouped", align_bytes=ALIGN)
                x2_grouped[b] = ring.tile([P, PAIRS * PACK], BF16, name="x2_grouped", align_bytes=ALIGN)
            picked = ring.tile([P, PAIRS], F32, name="picked")
            nc.vector.tensor_copy(picked[:], h[i][:].indirect(pos2_sb[:]))
            if i < GPSIMD_TILES:
                picked1 = ring.tile([P, PAIRS], F32, name="picked1")
                nc.vector.tensor_copy(picked1[:], h[i][:].indirect(pos1_sb[:]))
                nc.scalar.activation(picked[:], picked[:], ACT.Abs, scale=vecs[:, b, t : t + 1])
            else:
                nc.vector.tensor_copy(x1_planes[b][:, t, :], h[i][:].indirect(pos1_sb[:]))
                nc.scalar.activation(picked[:], picked[:], ACT.Abs)
            nc.scalar.activation(x2_planes[b][:, t, :], picked[:], ACT.Copy, scale=vecs[:, b, PACK + t : PACK + t + 1])
            if i < GPSIMD_TILES:
                nc.scalar.activation(x1_planes[b][:, t, :], picked1[:], ACT.Copy, scale=vecs[:, b, t : t + 1])
            if last and t == 1:
                interleave(x2_grouped[b], x2_planes[b], 0, 2, nc.scalar.copy)

        def mx_tiles(name):
            codes = keep.tile([P, PAIRS], U32, name=name + "_codes", align_bytes=ALIGN)
            scales = keep.tile([P, PAIRS], U8, name=name + "_sc", align_bytes=ALIGN)
            return codes, scales

        def quantise_x(grouped, codes, scales, cols=slice(0, PAIRS)):
            nc.vector.quantize_mx(
                out=codes[:, cols].bitcast(FP8X4),
                scales=scales[:, cols],
                in_=grouped[:, cols.start * PACK : cols.stop * PACK],
            )

        e_ps = []

        def second_stage(b):
            last = b == H_PASSES - 1
            x1_codes, x1_sc = mx_tiles("x1_%d" % b)
            x2_codes, x2_sc = mx_tiles("x2_%d" % b)
            if last:
                low, high = slice(0, PAIRS // 2), slice(PAIRS // 2, PAIRS)
                interleave(x2_grouped[b], x2_planes[b], 2, 4, nc.vector.tensor_copy)
                interleave(x1_grouped[b], x1_planes[b], 0, 4, nc.vector.tensor_copy, low)
                quantise_x(x2_grouped[b], x2_codes, x2_sc)
                quantise_x(x1_grouped[b], x1_codes, x1_sc, low)
                interleave(x1_grouped[b], x1_planes[b], 0, 4, nc.vector.tensor_copy, high)
                quantise_x(x1_grouped[b], x1_codes, x1_sc, high)
            else:
                quantise_x(x2_grouped[b], x2_codes, x2_sc)
                quantise_x(x1_grouped[b], x1_codes, x1_sc)
            for mt in range(PAIRS // P):
                if b == 0:
                    e_ps.append(psum.tile([P, PAIRS], F32, name="e_ps%d" % mt, tag="shared_bank"))
                nc.tensor.matmul_mx(
                    out=e_ps[mt][:],
                    lhsT=x1_codes[:, mt * P : (mt + 1) * P].bitcast(FP8X4),
                    lhsT_scale=x1_sc[:, mt * P : (mt + 1) * P],
                    rhs=x2_codes[:].bitcast(FP8X4),
                    rhs_scale=x2_sc[:],
                    start=(b == 0),
                    stop=last,
                )

        cosine(0)
        cosine(1)
        vec_ps = psum.tile([P, H_PASSES, P], F32, name="vec_ps", tag="a_ps")
        for b in range(H_PASSES):
            nc.tensor.transpose(vec_ps[:, b, :], vec_rows[:, b * P : (b + 1) * P], ident[:])
        vecs = keep.tile([P, H_PASSES, 2 * PACK], F32, name="vecs")
        nc.vector.tensor_copy(vecs[:], vec_ps[:, :, 0 : 2 * PACK])

        late = {(a, 0): round_w1_gpsimd(a, 1, 0) for a in (1, 0)}
        combine(0)
        for i in range(ROW_TILES):
            if i + 2 < ROW_TILES:
                cosine(i + 2)
            if i + 1 < ROW_TILES:
                combine(i + 1)
            if i == PACK:
                interleave(x2_grouped[0], x2_planes[0], 0, PACK, nc.scalar.copy)
            if i == PACK + 1:
                interleave(x1_grouped[0], x1_planes[0], 0, PACK, nc.scalar.copy)
            pick(i)
            if EARLY_TANH + i < ROW_TILES:
                tanh_product(EARLY_TANH + i)
            if i in (1, 2):
                late[i - 1, 1] = round_w1(i - 1, 1, 1, nc.scalar.copy)
            if i in (0, 3):
                for a in range(K_PASSES):
                    quantise_w1(a, 1, i // 3, late[a, i // 3])
            if i == PACK + 1:
                second_stage(0)
        second_stage(1)

        for mt in range(PAIRS // P):
            result = ring.tile([P, PAIRS], F32, name="result", bufs=4)
            nc.vector.tensor_tensor(result[:], e_ps[mt][:], shared_sb[:, mt, :], ALU.mult)
            nc.sync.dma_start(out[mt * P : (mt + 1) * P, :], result[:])
